import numpy as np
import ml_dtypes


def mxq(x, axis, fmt="e4m3"):
    dtype, down = {"e4m3": (ml_dtypes.float8_e4m3fn, 7), "e5m2": (ml_dtypes.float8_e5m2, 14)}[fmt]
    v = np.moveaxis(np.asarray(x, np.float32).astype(ml_dtypes.bfloat16).astype(np.float64), axis, -1)
    blocks = v.reshape(v.shape[:-1] + (-1, 32))
    amax = np.abs(blocks).max(-1, keepdims=True)
    byte = np.maximum(np.where(amax > 0, np.frexp(amax)[1] - 1 + 127, 0) - down, 1)
    scale = np.exp2(byte - 127.0)
    codes = (blocks / scale).astype(np.float32).astype(dtype).astype(np.float64)
    return np.moveaxis((codes * scale).reshape(v.shape), -1, axis)


WIDE = False


def mx_kscale(k):
    if not WIDE:
        return np.ones(k)
    levels = np.array([10, -10, 5, -5, 0])
    if k % 512:
        return np.exp2(np.random.permutation(np.resize(levels, k // 32))).repeat(32)
    a = np.empty((k // 512, 16))
    for p in range(k // 512):
        a[p, :8] = np.random.permutation(np.resize(levels, 8))
        for g in range(8):
            far = levels[np.abs(levels - a[p, g]) >= 10]
            a[p, g + 8] = far[np.random.randint(len(far))]
    return np.exp2(a.ravel()).repeat(32)


def f64(x):
    return np.asarray(x).astype(np.float64)


def striped(idx):
    return np.tile(idx.reshape(-1, 16).T, (8, 1)).astype(np.uint16)


def unstriped(offs):
    return offs[:16].T.reshape(-1).astype(np.int64)


E2M1 = np.array([0.0, 0.5, 1.0, 1.5, 2.0, 3.0, 4.0, 6.0, -0.0, -0.5, -1.0, -1.5, -2.0, -3.0, -4.0, -6.0])


def pack_weight(w, fmt):
    k, n = w.shape
    w = f64(np.asarray(w, np.float32).astype(ml_dtypes.bfloat16)).reshape(k // 32, 32, n)
    amax = np.abs(w).max(1)
    if fmt == "e4m3":
        byte = np.frexp(amax)[1] - 1 + 127 - 7
    else:
        mant, ex = np.frexp(amax / 6.0)
        byte = np.where(mant > 0.5, ex, ex - 1) + 127
    byte = np.clip(np.where(amax > 0, byte, 1), 1, 254)
    scaled = (w * np.exp2(127.0 - byte)[:, None, :]).reshape(k, n).astype(np.float32)
    by_word = np.ascontiguousarray(scaled.reshape(k // 512, 128, 4, n).transpose(0, 1, 3, 2))
    if fmt == "e4m3":
        words = by_word.astype(ml_dtypes.float8_e4m3fn).view(np.uint8)
    else:
        c = by_word.astype(ml_dtypes.float4_e2m1fn).view(np.uint8) & 0xF
        words = (c[..., 0::2] | (c[..., 1::2] << 4)).reshape(k // 512, 128, 2 * n)
    return np.ascontiguousarray(words), np.ascontiguousarray(byte.astype(np.uint8).reshape(k // 512, 16, n))


def unpack_weight(words, scales, fmt):
    g, _, n = scales.shape
    words = np.ascontiguousarray(words).reshape(g, 128, n, -1)
    if fmt == "e4m3":
        vals = words.view(ml_dtypes.float8_e4m3fn).astype(np.float64)
    else:
        nib = np.empty((g, 128, n, 4), np.uint8)
        nib[..., 0::2] = words & 0xF
        nib[..., 1::2] = words >> 4
        vals = E2M1[nib]
    vals = vals * np.repeat(np.exp2(scales.astype(np.float64) - 127.0), 8, axis=1)[..., None]
    return vals.transpose(0, 1, 3, 2).reshape(g * 512, n)


def pack_table(v):
    words, scales = pack_weight(v, "e4m3")
    return np.concatenate([words.reshape(words.shape[0], -1), scales.reshape(scales.shape[0], -1)], axis=1)


def unpack_table(tab):
    g, t = tab.shape[0], tab.shape[1] // 528
    return unpack_weight(tab[:, :512 * t].reshape(g, 128, t, 4), tab[:, 512 * t:].reshape(g, 16, t), "e4m3")


K, M, T, S = 1024, 256, 1024, 512


def setup_inputs():
    n = np.random.standard_normal
    s = mx_kscale(K)[:, None]
    w = n((K, M)) / np.sqrt(K) / s
    p_w4 = pack_weight(w[512:], "e2m1")
    return {
        "tab": pack_table(n((K, T)) * s),
        "w8": (w[:512]).astype(np.float32),
        "w4_words": p_w4[0],
        "w4_scales": p_w4[1],
        "wgo": np.tile(np.random.uniform(0.5, 2.0, S), (128, 1)).astype(np.float32),
        "offs": striped(np.random.permutation(T)[:S]),
        "offs2": striped(np.random.permutation(T)[:S]),
    }


def reference(tab, w8, w4_words, w4_scales, wgo, offs, offs2):
    tab_ = unpack_table(tab)[:, unstriped(offs)]
    w8_ = mxq(f64(w8), 0, "e4m3")
    w4_ = unpack_weight(w4_words, w4_scales, "e2m1")
    y = w8_.T @ tab_[:512] + w4_.T @ tab_[512:]
    out = np.zeros((M, T))
    out[:, unstriped(offs2)] = f64(wgo)[0] * (y)
    return out

from contextlib import ExitStack

import concourse.mybir as mybir

K, M, T, S = 1024, 256, 1024, 512
FLOPS = 2 * K * M * S

F32 = mybir.dt.float32
BF16 = mybir.dt.bfloat16
I32 = mybir.dt.int32
U32 = mybir.dt.uint32
U16 = mybir.dt.uint16
U8 = mybir.dt.uint8
E4M3 = mybir.dt.float8_e4m3fn_x4
E2M1 = mybir.dt.float4_e2m1fn_x4
MULT = mybir.AluOpType.mult

P = 128
PACK = 4
QUAD = 32
BLOCKS = M // P
HEAD = 128
PARTS = ((0, HEAD), (HEAD, S))


def widths(lo, hi, most):
    cuts = []
    while lo < hi:
        n = most
        while lo + n > hi:
            n //= 2
        cuts.append((lo, lo + n))
        lo += n
    return cuts


def tile_list_tabscat_o_none_kernel(tc, tab, w8, w4_words, w4_scales, wgo, offs, offs2, out):
    nc = tc.nc
    with ExitStack() as ctx:
        keep = ctx.enter_context(tc.tile_pool(name="keep", bufs=1))
        shared = ctx.enter_context(tc.tile_pool(name="shared", bufs=1))
        psum = ctx.enter_context(tc.psum_pool(name="psum", bufs=1))

        picks = keep.tile([P, S // 16], U16, name="picks")
        places = keep.tile([P, S // 16], U16, name="places")
        words = [keep.tile([P, T], U32, name=f"words{a}") for a in range(2)]
        tab_scales = keep.tile([P, 2, T], U8, name="tab_scales")
        w8_raw = shared.tile([P, PACK, M], F32, name="w8_raw", offset=0, align_bytes=64)
        w4_codes = keep.tile([P, 2 * M], U8, name="w4_codes", align_bytes=64)
        w4_plane = keep.tile([P, M], U8, name="w4_plane", align_bytes=64)
        weights = keep.tile([P, S], F32, name="weights")
        pages = [keep.tile([P, T], F32, name=f"page{b}") for b in range(BLOCKS)]

        def load_words(a):
            src = tab[a, 0 : 4 * P * T].bitcast(I32).rearrange("(p t) -> p t", p=P)
            nc.sync.dma_start(words[a][:].bitcast(I32), src)

        nc.vector.memset(tab_scales[:, 0, :].bitcast(I32), 0)
        nc.gpsimd.memset(tab_scales[:, 1, :].bitcast(I32), 0)
        nc.vector.memset(w4_plane[:].bitcast(I32), 0)
        for b in range(BLOCKS):
            nc.vector.memset(pages[b][:].bitcast(I32), 0)

        nc.sync.dma_start(picks[:], offs)
        load_words(0)
        for q in range(4):
            first = 4 * P * T + 4 * q * T
            src = tab[:, first : first + 4 * T].bitcast(I32).rearrange("a (r t) -> r a t", r=4)
            nc.sync.dma_start(tab_scales[QUAD * q : QUAD * q + 4, :, :].bitcast(I32), src)
        nc.sync.dma_start(w8_raw[:], w8.rearrange("(p j) n -> p j n", j=PACK))
        load_words(1)
        nc.sync.dma_start(w4_codes[:].bitcast(I32), w4_words[0].bitcast(I32))
        for q in range(4):
            nc.sync.dma_start(
                w4_plane[QUAD * q : QUAD * q + 4, :].bitcast(I32), w4_scales[0, 4 * q : 4 * q + 4, :].bitcast(I32)
            )
        nc.sync.dma_start(places[:], offs2)
        nc.sync.dma_start(weights[:], wgo)

        got0 = keep.tile([P, S], U32, name="got0", align_bytes=64)
        nc.vector.tensor_copy(got0[:], words[0][:].indirect(picks[:]))
        scales0 = keep.tile([P, S], U8, name="scales0", align_bytes=64)
        nc.vector.tensor_copy(scales0[:], tab_scales[:, 0, :].indirect(picks[:]))

        w8_codes, w8_planes = [], []
        for b in range(BLOCKS):
            grouped = keep.tile([P, P, PACK], BF16, name=f"grouped{b}", align_bytes=64)
            nc.scalar.copy(
                grouped[:].rearrange("p (c i) t -> p c t i", i=4),
                w8_raw[:, :, b * P : (b + 1) * P].rearrange("p t (c i) -> p c t i", i=4),
            )
            codes = keep.tile([P, P], U32, name=f"w8_codes{b}", align_bytes=64)
            plane = keep.tile([P, P], U8, name=f"w8_plane{b}", align_bytes=64)
            nc.vector.quantize_mx(
                out=codes[:].bitcast(E4M3), scales=plane[:], in_=grouped[:].rearrange("p n t -> p (n t)")
            )
            w8_codes.append(codes)
            w8_planes.append(plane)

        got1, scales1 = [], []
        for i, (lo, hi) in enumerate(PARTS):
            listed = picks[:, lo // 16 : hi // 16]
            if i == 0:
                plane = keep.tile([P, hi - lo], U8, name="scales1_head", align_bytes=64)
            else:
                plane = shared.tile([P, hi - lo], U8, name="scales1_rest", offset=4 * S, align_bytes=64)
            nc.vector.tensor_copy(plane[:], tab_scales[:, 1, :].indirect(listed))
            part = shared.tile([P, hi - lo], U32, name=f"got1_{i}", offset=4 * lo, align_bytes=64)
            nc.vector.tensor_copy(part[:], words[1][:].indirect(listed))
            scales1.append(plane)
            got1.append(part)

        sums = {}
        for i, (lo, hi) in enumerate(PARTS):
            for b in range(BLOCKS):
                acc = psum.tile([P, hi - lo], F32, name=f"acc{i}_{b}")
                for c0, c1 in widths(lo, hi, 256):
                    nc.tensor.matmul_mx(
                        out=acc[:, c0 - lo : c1 - lo],
                        lhsT=w8_codes[b][:].bitcast(E4M3),
                        lhsT_scale=w8_planes[b][:],
                        rhs=got0[:, c0:c1].bitcast(E4M3),
                        rhs_scale=scales0[:, c0:c1],
                        start=(c0 == lo),
                        stop=False,
                    )
                for c0, c1 in widths(0, hi - lo, 128):
                    nc.tensor.matmul_mx(
                        out=acc[:, c0:c1],
                        lhsT=w4_codes[:, 2 * b * P : 2 * (b + 1) * P].bitcast(E2M1),
                        lhsT_scale=w4_plane[:, b * P : (b + 1) * P],
                        rhs=got1[i][:, c0:c1].bitcast(E4M3),
                        rhs_scale=scales1[i][:, c0:c1],
                        start=False,
                        stop=(c1 == hi - lo),
                    )
                y = keep.tile([P, hi - lo], F32, name=f"y{i}_{b}")
                nc.scalar.copy(y[:], acc[:])
                sums[i, b] = y

        for i, (lo, hi) in enumerate(PARTS):
            for b in range(BLOCKS):
                nc.vector.tensor_tensor(
                    pages[b][:].indirect(places[:, lo // 16 : hi // 16]), sums[i, b][:], weights[:, lo:hi], MULT
                )
        for b in range(BLOCKS):
            nc.sync.dma_start(out[b * P : (b + 1) * P, :], pages[b][:])
